import numpy as np
import ml_dtypes


def mxq(x, axis, fmt="e4m3"):
    dtype, down = {"e4m3": (ml_dtypes.float8_e4m3fn, 7), "e5m2": (ml_dtypes.float8_e5m2, 14)}[fmt]
    v = np.moveaxis(np.asarray(x, np.float32).astype(ml_dtypes.bfloat16).astype(np.float64), axis, -1)
    blocks = v.reshape(v.shape[:-1] + (-1, 32))
    amax = np.abs(blocks).max(-1, keepdims=True)
    byte = np.maximum(np.where(amax > 0, np.frexp(amax)[1] - 1 + 127, 0) - down, 1)
    scale = np.exp2(byte - 127.0)
    codes = (blocks / scale).astype(np.float32).astype(dtype).astype(np.float64)
    return np.moveaxis((codes * scale).reshape(v.shape), -1, axis)


WIDE = False


def mx_kscale(k):
    if not WIDE:
        return np.ones(k)
    levels = np.array([10, -10, 5, -5, 0])
    if k % 512:
        return np.exp2(np.random.permutation(np.resize(levels, k // 32))).repeat(32)
    a = np.empty((k // 512, 16))
    for p in range(k // 512):
        a[p, :8] = np.random.permutation(np.resize(levels, 8))
        for g in range(8):
            far = levels[np.abs(levels - a[p, g]) >= 10]
            a[p, g + 8] = far[np.random.randint(len(far))]
    return np.exp2(a.ravel()).repeat(32)


def f64(x):
    return np.asarray(x).astype(np.float64)


def striped(idx):
    return np.tile(idx.reshape(-1, 16).T, (8, 1)).astype(np.uint16)


def unstriped(offs):
    return offs[:16].T.reshape(-1).astype(np.int64)


def pack_weight(w):
    k, n = w.shape
    w = f64(np.asarray(w, np.float32).astype(ml_dtypes.bfloat16)).reshape(k // 32, 32, n)
    amax = np.abs(w).max(1)
    byte = np.clip(np.where(amax > 0, np.frexp(amax)[1] - 1 + 127 - 7, 1), 1, 254)
    scaled = (w * np.exp2(127.0 - byte)[:, None, :]).reshape(k, n).astype(np.float32)
    words = np.ascontiguousarray(scaled.reshape(k // 512, 128, 4, n).transpose(0, 1, 3, 2)).astype(ml_dtypes.float8_e4m3fn).view(np.uint8)
    return words, np.ascontiguousarray(byte.astype(np.uint8).reshape(k // 512, 16, n))


def unpack_weight(words, scales):
    g, p, n, _ = words.shape
    vals = np.ascontiguousarray(words).view(ml_dtypes.float8_e4m3fn).astype(np.float64) * np.repeat(np.exp2(scales.astype(np.float64) - 127.0), 8, axis=1)[..., None]
    return vals.transpose(0, 1, 3, 2).reshape(g * 512, n)


def sigmoid(v):
    return 1.0 / (1.0 + np.exp(-np.maximum(v, -700.0)))


K, T, S, H, U, J = 512, 2048, 512, 512, 1024, 512


def setup_inputs():
    n = np.random.standard_normal
    s = mx_kscale(K)[:, None]
    u = mx_kscale(H)
    packed_xT = pack_weight(n((K, T)) * s)
    return {
        "x_words": packed_xT[0],
        "x_scales": packed_xT[1],
        "mem": (n((H, U)) * u[:, None]).astype(np.float32),
        "w1": (n((K, H)) / np.sqrt(2 * K) / s).astype(np.float32),
        "w2": (n((K, H)) / np.sqrt(2 * K) / s).astype(np.float32),
        "r1": (n((H, J)) / np.sqrt(2 * H) / u[:, None]).astype(np.float32),
        "r2": (n((H, J)) / np.sqrt(2 * H) / u[:, None]).astype(np.float32),
        "unit": (np.random.uniform(0.6, 1.4, (H, 1)) / u[:, None]).astype(np.float32),
        "offs": striped(np.random.permutation(T)[:S]),
        "slot": striped(np.random.permutation(U)[:S]),
    }


def reference(x_words, x_scales, mem, w1, w2, r1, r2, unit, offs, slot):
    old = f64(mem)[:, unstriped(slot)]
    ov = f64(unit) * old
    xq = unpack_weight(x_words, x_scales)[:, unstriped(offs)]
    oldq = mxq(old, 0, "e4m3")
    z = sigmoid(mxq(f64(w1), 0, "e4m3").T @ xq + mxq(f64(r1), 0, "e4m3").T @ oldq)
    gg = np.tanh(mxq(f64(w2), 0, "e4m3").T @ xq + mxq(f64(r2), 0, "e4m3").T @ oldq)
    return ov * z + gg

@@ -1,0 +1,204 @@
+from contextlib import ExitStack
+
+import concourse.mybir as mybir
+
+K, T, S, H, U = 512, 2048, 512, 512, 1024
+FLOPS = 4 * 2 * K * H * S
+
+F32 = mybir.dt.float32
+BF16 = mybir.dt.bfloat16
+I32 = mybir.dt.int32
+U32 = mybir.dt.uint32
+U16 = mybir.dt.uint16
+U8 = mybir.dt.uint8
+FP8X4 = mybir.dt.float8_e4m3fn_x4
+ACT = mybir.ActivationFunctionType
+ALU = mybir.AluOpType
+
+P = 128
+PACK = 4
+
+
+def tile_picked_ytgn_fg_p_kernel(
+    tc, x_words, x_scales, mem, w1, w2, r1, r2, unit, offs, slot, out
+):
+    nc = tc.nc
+    with ExitStack() as ctx:
+        keep = ctx.enter_context(tc.tile_pool(name="keep", bufs=1))
+        psum = ctx.enter_context(tc.psum_pool(name="psum", bufs=1))
+        copies = (nc.vector.tensor_copy, nc.scalar.copy)
+
+        def load_weight(w, name, pieces):
+            rows = w.rearrange("(p j) c -> p j c", j=PACK)
+            width = H // pieces
+            raw = []
+            for a in range(pieces):
+                piece = keep.tile([P, PACK, width], F32, name="%s_raw%d" % (name, a))
+                nc.sync.dma_start(out=piece[:], in_=rows[:, :, a * width : (a + 1) * width])
+                raw.append(piece)
+            return raw
+
+        def load_half(w, name, a):
+            piece = keep.tile([P, PACK, H // 2], F32, name="%s_raw%d" % (name, a))
+            nc.sync.dma_start(out=piece[:], in_=w.rearrange("(p j) c -> p j c", j=PACK)[:, :, a * 256 : (a + 1) * 256])
+            return piece
+
+        def dealt_tiles(name):
+            return [keep.tile([P, 2, P, PACK], BF16, name="%s_dealt%d" % (name, u), tag="dealt%d" % u, align_bytes=64) for u in range(2)]
+
+        def deal(dealt, raw, a, engines=(0, 1)):
+            n = P // len(raw)
+            for u in range(2):
+                copies[engines[u]](
+                    out=dealt[u][:, :, a * n : (a + 1) * n, :].rearrange("p t m j -> p m j t"),
+                    in_=raw[a][:].rearrange("p j (m t) -> p m j t", t=PACK)[:, :, :, 2 * u : 2 * u + 2],
+                )
+
+        def mx_tiles(name):
+            codes = keep.tile([P, 512], U32, name=name + "_codes", align_bytes=64)
+            scales = keep.tile([P, 512], U8, name=name + "_scales", align_bytes=64)
+            return codes, scales
+
+        def quantize(mx, c0, c1, values):
+            nc.vector.quantize_mx(out=mx[0][:, c0:c1].bitcast(FP8X4), scales=mx[1][:, c0:c1], in_=values)
+
+        def quantize_weight(name, dealt, fine=False):
+            mx = mx_tiles(name)
+            for u in range(2):
+                if fine:
+                    for v in range(2):
+                        t = 2 * u + v
+                        quantize(mx, t * P, (t + 1) * P, dealt[u][:, v].rearrange("p m j -> p (m j)"))
+                else:
+                    quantize(mx, 2 * u * P, 2 * (u + 1) * P, dealt[u][:].rearrange("p t m j -> p (t m j)"))
+            return mx
+
+        def product(bank, t, weight, moving, start):
+            cols = slice(t * P, (t + 1) * P)
+            nc.tensor.matmul_mx(
+                out=bank[:],
+                lhsT=weight[0][:, cols].bitcast(FP8X4),
+                lhsT_scale=weight[1][:, cols],
+                rhs=moving[0][:].bitcast(FP8X4),
+                rhs_scale=moving[1][:],
+                start=start,
+                stop=not start,
+            )
+
+        offs_t = keep.tile([P, S // 16], U16, name="offs_t")
+        slot_t = keep.tile([P, S // 16], U16, name="slot_t")
+        scale_table = keep.tile([P, T], U8, name="scale_table")
+        nc.vector.memset(scale_table[:].bitcast(I32), 0)
+
+        mem_rows = mem.rearrange("(p t) u -> p t u", t=PACK)
+
+        def load_plane(t):
+            plane = keep.tile([P, U], F32, name="mem_plane%d" % t)
+            nc.sync.dma_start(out=plane[:], in_=mem_rows[:, t, :])
+            return plane
+
+        def load_words():
+            table = keep.tile([P, T], I32, name="word_table")
+            nc.sync.dma_start(out=table[:], in_=x_words[0].rearrange("p n t -> p (n t)").bitcast(I32))
+            return table
+
+        nc.sync.dma_start(slot_t[:], slot)
+        mem_planes = [load_plane(0), load_plane(1)]
+        for q in range(4):
+            nc.sync.dma_start(
+                out=scale_table[32 * q : 32 * q + 4, :].bitcast(I32),
+                in_=x_scales[0, 4 * q : 4 * q + 4, :].bitcast(I32),
+            )
+        nc.sync.dma_start(offs_t[:], offs)
+        mem_planes.append(load_plane(2))
+        r1_raw = [load_half(r1, "r1", 0)]
+        mem_planes.append(load_plane(3))
+        r1_raw.append(load_half(r1, "r1", 1))
+        word_table = load_words()
+        w1_raw = load_weight(w1, "w1", 2)
+        unit_t = keep.tile([P, PACK], F32, name="unit_t")
+        nc.sync.dma_start(out=unit_t[:], in_=unit.rearrange("(p t) o -> p (t o)", t=PACK))
+        r2_raw = load_weight(r2, "r2", 2)
+        w2_raw = load_weight(w2, "w2", 2)
+
+        gate_bank = [psum.tile([P, S], F32, name="gate_bank%d" % t) for t in range(PACK)]
+        cand_bank = [psum.tile([P, S], F32, name="cand_bank%d" % t) for t in range(PACK)]
+
+        old = keep.tile([P, PACK, S], F32, name="old")
+
+        def look_up(t):
+            nc.vector.tensor_copy(old[:, t, :], mem_planes[t][:].indirect(slot_t[:]))
+
+        look_up(0)
+        look_up(1)
+        look_up(2)
+        x_scale = keep.tile([P, S], U8, name="x_scale", align_bytes=64)
+        nc.vector.tensor_copy(x_scale[:], scale_table[:].indirect(offs_t[:]))
+        r1_dealt = dealt_tiles("r1")
+        deal(r1_dealt, r1_raw, 0, (1, 1))
+        look_up(3)
+        deal(r1_dealt, r1_raw, 1, (1, 1))
+
+        old_mx = mx_tiles("old")
+        woven = []
+        for u in range(2):
+            half = keep.tile([P, S // 2, PACK], BF16, name="woven%d" % u, align_bytes=64)
+            copies[u](
+                out=half[:].rearrange("p (c i) t -> p c t i", i=4),
+                in_=old[:, :, u * 256 : (u + 1) * 256].rearrange("p t (c i) -> p c t i", i=4),
+            )
+            woven.append(half)
+        quantize(old_mx, 0, 256, woven[0][:].rearrange("p s t -> p (s t)"))
+        r1_mx = quantize_weight("r1", r1_dealt)
+        quantize(old_mx, 256, 512, woven[1][:].rearrange("p s t -> p (s t)"))
+        for t in range(PACK):
+            product(gate_bank[t], t, r1_mx, old_mx, True)
+
+        x_code = keep.tile([P, S], U32, name="x_code", align_bytes=64)
+        x_mx = (x_code, x_scale)
+        nc.vector.tensor_copy(x_code[:], word_table[:].bitcast(U32).indirect(offs_t[:]))
+
+        w1_dealt = dealt_tiles("w1")
+        for a in range(len(w1_raw)):
+            deal(w1_dealt, w1_raw, a)
+        w1_mx = quantize_weight("w1", w1_dealt)
+
+        gate = [keep.tile([P, S], F32, name="gate%d" % t) for t in range(PACK)]
+        kept = [keep.tile([P, S], F32, name="kept%d" % t) for t in range(PACK)]
+
+        def open_gate(t):
+            product(gate_bank[t], t, w1_mx, x_mx, False)
+            nc.scalar.activation(out=gate[t][:], in_=gate_bank[t][:], func=ACT.Sigmoid)
+
+        def forget(t):
+            nc.vector.scalar_tensor_tensor(
+                out=kept[t][:], in0=old[:, t, :], scalar=unit_t[:, t : t + 1], in1=gate[t][:], op0=ALU.mult, op1=ALU.mult
+            )
+
+        r2_dealt = dealt_tiles("r2")
+        deal(r2_dealt, r2_raw, 0)
+        open_gate(0)
+        open_gate(1)
+        deal(r2_dealt, r2_raw, 1)
+        forget(0)
+        open_gate(2)
+        r2_mx = quantize_weight("r2", r2_dealt)
+        open_gate(3)
+        for t in range(PACK):
+            product(cand_bank[t], t, r2_mx, old_mx, True)
+        forget(1)
+        w2_dealt = dealt_tiles("w2")
+        deal(w2_dealt, w2_raw, 0)
+        forget(2)
+        deal(w2_dealt, w2_raw, 1)
+        w2_mx = quantize_weight("w2", w2_dealt, True)
+        forget(3)
+
+        out_rows = out.rearrange("(p t) s -> p t s", t=PACK)
+        for t in range(PACK):
+            product(cand_bank[t], t, w2_mx, x_mx, False)
+            cand = keep.tile([P, S], F32, name="cand%d" % t)
+            nc.scalar.activation(out=cand[:], in_=cand_bank[t][:], func=ACT.Tanh)
+            res = keep.tile([P, S], F32, name="res%d" % t)
+            nc.vector.tensor_tensor(out=res[:], in0=kept[t][:], in1=cand[:], op=ALU.add)
+            nc.sync.dma_start(out=out_rows[:, t, :], in_=res[:])

@@ -28,23 +28,13 @@ def tile_picked_ytgn_fg_p_kernel(
         psum = ctx.enter_context(tc.psum_pool(name="psum", bufs=1))
         copies = (nc.vector.tensor_copy, nc.scalar.copy)
 
-        def load_weight(w, name, pieces):
-            rows = w.rearrange("(p j) c -> p j c", j=PACK)
-            width = H // pieces
-            raw = []
-            for a in range(pieces):
-                piece = keep.tile([P, PACK, width], F32, name="%s_raw%d" % (name, a))
-                nc.sync.dma_start(out=piece[:], in_=rows[:, :, a * width : (a + 1) * width])
-                raw.append(piece)
-            return raw
-
         def load_half(w, name, a):
-            piece = keep.tile([P, PACK, H // 2], F32, name="%s_raw%d" % (name, a))
+            piece = keep.tile([P, PACK, H // 2], F32, name="%s_raw%d" % (name, a), tag="%s_raw%d" % (name, a), align_bytes=64)
             nc.sync.dma_start(out=piece[:], in_=w.rearrange("(p j) c -> p j c", j=PACK)[:, :, a * 256 : (a + 1) * 256])
             return piece
 
         def dealt_tiles(name):
-            return [keep.tile([P, 2, P, PACK], BF16, name="%s_dealt%d" % (name, u), tag="dealt%d" % u, align_bytes=64) for u in range(2)]
+            return [keep.tile([P, 2, P, PACK], BF16, name="%s_dealt%d" % (name, u), tag="%s_dealt%d" % (name, u), align_bytes=64) for u in range(2)]
 
         def deal(dealt, raw, a, engines=(0, 1)):
             n = P // len(raw)
@@ -89,6 +79,10 @@ def tile_picked_ytgn_fg_p_kernel(
         slot_t = keep.tile([P, S // 16], U16, name="slot_t")
         scale_table = keep.tile([P, T], U8, name="scale_table")
         nc.vector.memset(scale_table[:].bitcast(I32), 0)
+        warm = keep.tile([P, 8], F32, name="warm")
+        nc.vector.memset(warm[:], 0.0)
+        warm_out = keep.tile([P, 8], F32, name="warm_out")
+        nc.scalar.activation(out=warm_out[:], in_=warm[:], func=ACT.Sigmoid)
 
         mem_rows = mem.rearrange("(p t) u -> p t u", t=PACK)
 
@@ -97,10 +91,12 @@ def tile_picked_ytgn_fg_p_kernel(
             nc.sync.dma_start(out=plane[:], in_=mem_rows[:, t, :])
             return plane
 
-        def load_words():
-            table = keep.tile([P, T], I32, name="word_table")
-            nc.sync.dma_start(out=table[:], in_=x_words[0].rearrange("p n t -> p (n t)").bitcast(I32))
-            return table
+        word_table = keep.tile([P, T], I32, name="word_table")
+        word_rows = x_words[0].rearrange("p n t -> p (n t)").bitcast(I32)
+
+        def load_words(a):
+            cols = slice(a * T // 2, (a + 1) * T // 2)
+            nc.sync.dma_start(out=word_table[:, cols], in_=word_rows[:, cols])
 
         nc.sync.dma_start(slot_t[:], slot)
         mem_planes = [load_plane(0), load_plane(1)]
@@ -114,12 +110,13 @@ def tile_picked_ytgn_fg_p_kernel(
         r1_raw = [load_half(r1, "r1", 0)]
         mem_planes.append(load_plane(3))
         r1_raw.append(load_half(r1, "r1", 1))
-        word_table = load_words()
-        w1_raw = load_weight(w1, "w1", 2)
+        load_words(0)
+        load_words(1)
+        w1_raw = [load_half(w1, "w1", a) for a in range(2)]
         unit_t = keep.tile([P, PACK], F32, name="unit_t")
         nc.sync.dma_start(out=unit_t[:], in_=unit.rearrange("(p t) o -> p (t o)", t=PACK))
-        r2_raw = load_weight(r2, "r2", 2)
-        w2_raw = load_weight(w2, "w2", 2)
+        r2_raw = [load_half(r2, "r2", a) for a in range(2)]
+        w2_raw = [load_half(w2, "w2", a) for a in range(2)]
 
         gate_bank = [psum.tile([P, S], F32, name="gate_bank%d" % t) for t in range(PACK)]
         cand_bank = [psum.tile([P, S], F32, name="cand_bank%d" % t) for t in range(PACK)]
@@ -129,9 +126,8 @@ def tile_picked_ytgn_fg_p_kernel(
         def look_up(t):
             nc.vector.tensor_copy(old[:, t, :], mem_planes[t][:].indirect(slot_t[:]))
 
-        look_up(0)
-        look_up(1)
-        look_up(2)
+        for t in range(3):
+            look_up(t)
         x_scale = keep.tile([P, S], U8, name="x_scale", align_bytes=64)
         nc.vector.tensor_copy(x_scale[:], scale_table[:].indirect(offs_t[:]))
         r1_dealt = dealt_tiles("r1")
@@ -142,56 +138,58 @@ def tile_picked_ytgn_fg_p_kernel(
         old_mx = mx_tiles("old")
         woven = []
         for u in range(2):
-            half = keep.tile([P, S // 2, PACK], BF16, name="woven%d" % u, align_bytes=64)
+            half = keep.tile([P, S // 2, PACK], BF16, name="woven%d" % u, tag=("woven0", "r1_raw1")[u], align_bytes=64)
             copies[u](
                 out=half[:].rearrange("p (c i) t -> p c t i", i=4),
                 in_=old[:, :, u * 256 : (u + 1) * 256].rearrange("p t (c i) -> p c t i", i=4),
             )
             woven.append(half)
-        quantize(old_mx, 0, 256, woven[0][:].rearrange("p s t -> p (s t)"))
         r1_mx = quantize_weight("r1", r1_dealt)
-        quantize(old_mx, 256, 512, woven[1][:].rearrange("p s t -> p (s t)"))
+        for u in range(2):
+            quantize(old_mx, u * 256, (u + 1) * 256, woven[u][:].rearrange("p s t -> p (s t)"))
+        x_code = keep.tile([P, S], U32, name="x_code", tag="r1_raw1", align_bytes=64)
+        x_mx = (x_code, x_scale)
+        nc.vector.tensor_copy(x_code[:], word_table[:].bitcast(U32).indirect(offs_t[:]))
         for t in range(PACK):
             product(gate_bank[t], t, r1_mx, old_mx, True)
 
-        x_code = keep.tile([P, S], U32, name="x_code", align_bytes=64)
-        x_mx = (x_code, x_scale)
-        nc.vector.tensor_copy(x_code[:], word_table[:].bitcast(U32).indirect(offs_t[:]))
-
         w1_dealt = dealt_tiles("w1")
-        for a in range(len(w1_raw)):
+        for a in range(2):
             deal(w1_dealt, w1_raw, a)
         w1_mx = quantize_weight("w1", w1_dealt)
 
-        gate = [keep.tile([P, S], F32, name="gate%d" % t) for t in range(PACK)]
-        kept = [keep.tile([P, S], F32, name="kept%d" % t) for t in range(PACK)]
+        gate, kept = {}, {}
+        gate_tag = ["gate0", "gate1", "w2_raw0", "w2_raw1"]
+        kept_tag = ["kept0", "kept1", "w2_dealt0", "w2_dealt1"]
 
         def open_gate(t):
             product(gate_bank[t], t, w1_mx, x_mx, False)
+            gate[t] = keep.tile([P, S], F32, name="gate%d" % t, tag=gate_tag[t], align_bytes=64)
             nc.scalar.activation(out=gate[t][:], in_=gate_bank[t][:], func=ACT.Sigmoid)
 
         def forget(t):
+            kept[t] = keep.tile([P, S], F32, name="kept%d" % t, tag=kept_tag[t], align_bytes=64)
             nc.vector.scalar_tensor_tensor(
                 out=kept[t][:], in0=old[:, t, :], scalar=unit_t[:, t : t + 1], in1=gate[t][:], op0=ALU.mult, op1=ALU.mult
             )
 
         r2_dealt = dealt_tiles("r2")
-        deal(r2_dealt, r2_raw, 0)
+        deal(r2_dealt, r2_raw, 0, (0, 0))
         open_gate(0)
-        open_gate(1)
         deal(r2_dealt, r2_raw, 1)
         forget(0)
-        open_gate(2)
         r2_mx = quantize_weight("r2", r2_dealt)
-        open_gate(3)
+        open_gate(1)
         for t in range(PACK):
             product(cand_bank[t], t, r2_mx, old_mx, True)
         forget(1)
         w2_dealt = dealt_tiles("w2")
-        deal(w2_dealt, w2_raw, 0)
-        forget(2)
+        deal(w2_dealt, w2_raw, 0, (1, 1))
+        open_gate(2)
         deal(w2_dealt, w2_raw, 1)
         w2_mx = quantize_weight("w2", w2_dealt, True)
+        open_gate(3)
+        forget(2)
         forget(3)
 
         out_rows = out.rearrange("(p t) s -> p t s", t=PACK)
@@ -199,6 +197,9 @@ def tile_picked_ytgn_fg_p_kernel(
             product(cand_bank[t], t, w2_mx, x_mx, False)
             cand = keep.tile([P, S], F32, name="cand%d" % t)
             nc.scalar.activation(out=cand[:], in_=cand_bank[t][:], func=ACT.Tanh)
-            res = keep.tile([P, S], F32, name="res%d" % t)
-            nc.vector.tensor_tensor(out=res[:], in0=kept[t][:], in1=cand[:], op=ALU.add)
-            nc.sync.dma_start(out=out_rows[:, t, :], in_=res[:])
+            pieces = 2 if t == PACK - 1 else 1
+            for a in range(pieces):
+                cols = slice(a * S // pieces, (a + 1) * S // pieces)
+                res = keep.tile([P, S // pieces], F32, name="res%d_%d" % (t, a))
+                nc.vector.tensor_tensor(out=res[:], in0=kept[t][:, cols], in1=cand[:, cols], op=ALU.add)
+                nc.sync.dma_start(out=out_rows[:, t, cols], in_=res[:])

@@ -40,8 +40,8 @@ def tile_picked_ytgn_fg_p_kernel(
             n = P // len(raw)
             for u in range(2):
                 copies[engines[u]](
-                    out=dealt[u][:, :, a * n : (a + 1) * n, :].rearrange("p t m j -> p m j t"),
-                    in_=raw[a][:].rearrange("p j (m t) -> p m j t", t=PACK)[:, :, :, 2 * u : 2 * u + 2],
+                    out=dealt[u][:, :, a * n : (a + 1) * n, :].rearrange("p t m j -> p m t j"),
+                    in_=raw[a][:].rearrange("p j (m t) -> p m t j", t=PACK)[:, :, 2 * u : 2 * u + 2, :],
                 )
 
         def mx_tiles(name):
@@ -100,11 +100,9 @@ def tile_picked_ytgn_fg_p_kernel(
 
         nc.sync.dma_start(slot_t[:], slot)
         mem_planes = [load_plane(0), load_plane(1)]
-        for q in range(4):
-            nc.sync.dma_start(
-                out=scale_table[32 * q : 32 * q + 4, :].bitcast(I32),
-                in_=x_scales[0, 4 * q : 4 * q + 4, :].bitcast(I32),
-            )
+        scale_rows = x_scales[0].bitcast(I32).rearrange("(q r) c -> r q c", r=4)
+        for r in range(4):
+            nc.sync.dma_start(out=scale_table[r : P : 32, :].bitcast(I32), in_=scale_rows[r])
         nc.sync.dma_start(offs_t[:], offs)
         mem_planes.append(load_plane(2))
         r1_raw = [load_half(r1, "r1", 0)]
@@ -140,8 +138,8 @@ def tile_picked_ytgn_fg_p_kernel(
         for u in range(2):
             half = keep.tile([P, S // 2, PACK], BF16, name="woven%d" % u, tag=("woven0", "r1_raw1")[u], align_bytes=64)
             copies[u](
-                out=half[:].rearrange("p (c i) t -> p c t i", i=4),
-                in_=old[:, :, u * 256 : (u + 1) * 256].rearrange("p t (c i) -> p c t i", i=4),
+                out=half[:],
+                in_=old[:, :, u * 256 : (u + 1) * 256].rearrange("p t s -> p s t"),
             )
             woven.append(half)
         r1_mx = quantize_weight("r1", r1_dealt)

@@ -17,6 +17,8 @@ ALU = mybir.AluOpType
 
 P = 128
 PACK = 4
+PAIRS = 2
+LINE = 4
 
 
 def tile_picked_ytgn_fg_p_kernel(
@@ -26,42 +28,28 @@ def tile_picked_ytgn_fg_p_kernel(
     with ExitStack() as ctx:
         keep = ctx.enter_context(tc.tile_pool(name="keep", bufs=1))
         psum = ctx.enter_context(tc.psum_pool(name="psum", bufs=1))
-        copies = (nc.vector.tensor_copy, nc.scalar.copy)
 
-        def load_half(w, name, a):
-            piece = keep.tile([P, PACK, H // 2], F32, name="%s_raw%d" % (name, a), tag="%s_raw%d" % (name, a), align_bytes=64)
-            nc.sync.dma_start(out=piece[:], in_=w.rearrange("(p j) c -> p j c", j=PACK)[:, :, a * 256 : (a + 1) * 256])
-            return piece
+        def load_weight(w, name):
+            raw = keep.tile([P, PACK, H], F32, name=name + "_raw", tag=name + "_raw", align_bytes=64)
+            nc.sync.dma_start(out=raw[:], in_=w.rearrange("(p j) c -> p j c", j=PACK))
+            return raw
 
-        def dealt_tiles(name):
-            return [keep.tile([P, 2, P, PACK], BF16, name="%s_dealt%d" % (name, u), tag="%s_dealt%d" % (name, u), align_bytes=64) for u in range(2)]
-
-        def deal(dealt, raw, a, engines=(0, 1)):
-            n = P // len(raw)
-            for u in range(2):
-                copies[engines[u]](
-                    out=dealt[u][:, :, a * n : (a + 1) * n, :].rearrange("p t m j -> p m t j"),
-                    in_=raw[a][:].rearrange("p j (m t) -> p m t j", t=PACK)[:, :, 2 * u : 2 * u + 2, :],
-                )
+        def deal(copy, raw, u, tag):
+            dealt = keep.tile([P, 2, P, PACK], BF16, name="dealt", tag=tag, align_bytes=64)
+            copy(
+                out=dealt[:].rearrange("p v m j -> p m j v"),
+                in_=raw[:].rearrange("p j (m t) -> p m j t", t=PACK)[:, :, :, 2 * u : 2 * u + 2],
+            )
+            return dealt[:].rearrange("p v m j -> p (v m j)")
 
         def mx_tiles(name):
-            codes = keep.tile([P, 512], U32, name=name + "_codes", align_bytes=64)
-            scales = keep.tile([P, 512], U8, name=name + "_scales", align_bytes=64)
+            codes = keep.tile([P, S], U32, name=name + "_codes", align_bytes=64)
+            scales = keep.tile([P, S], U8, name=name + "_scales", align_bytes=64)
             return codes, scales
 
-        def quantize(mx, c0, c1, values):
-            nc.vector.quantize_mx(out=mx[0][:, c0:c1].bitcast(FP8X4), scales=mx[1][:, c0:c1], in_=values)
-
-        def quantize_weight(name, dealt, fine=False):
-            mx = mx_tiles(name)
-            for u in range(2):
-                if fine:
-                    for v in range(2):
-                        t = 2 * u + v
-                        quantize(mx, t * P, (t + 1) * P, dealt[u][:, v].rearrange("p m j -> p (m j)"))
-                else:
-                    quantize(mx, 2 * u * P, 2 * (u + 1) * P, dealt[u][:].rearrange("p t m j -> p (t m j)"))
-            return mx
+        def quantize(mx, first, values):
+            cols = slice(first, first + values.shape[1] // PACK)
+            nc.vector.quantize_mx(out=mx[0][:, cols].bitcast(FP8X4), scales=mx[1][:, cols], in_=values)
 
         def product(bank, t, weight, moving, start):
             cols = slice(t * P, (t + 1) * P)
@@ -85,110 +73,96 @@ def tile_picked_ytgn_fg_p_kernel(
         nc.scalar.activation(out=warm_out[:], in_=warm[:], func=ACT.Sigmoid)
 
         mem_rows = mem.rearrange("(p t) u -> p t u", t=PACK)
-
-        def load_plane(t):
-            plane = keep.tile([P, U], F32, name="mem_plane%d" % t)
-            nc.sync.dma_start(out=plane[:], in_=mem_rows[:, t, :])
-            return plane
-
-        word_table = keep.tile([P, T], I32, name="word_table")
-        word_rows = x_words[0].rearrange("p n t -> p (n t)").bitcast(I32)
-
-        def load_words(a):
-            cols = slice(a * T // 2, (a + 1) * T // 2)
-            nc.sync.dma_start(out=word_table[:, cols], in_=word_rows[:, cols])
-
+        mem_planes = [keep.tile([P, U], F32, name="mem_plane%d" % t) for t in range(PACK)]
         nc.sync.dma_start(slot_t[:], slot)
-        mem_planes = [load_plane(0), load_plane(1)]
-        scale_rows = x_scales[0].bitcast(I32).rearrange("(q r) c -> r q c", r=4)
-        for r in range(4):
-            nc.sync.dma_start(out=scale_table[r : P : 32, :].bitcast(I32), in_=scale_rows[r])
+        for t in range(PACK):
+            nc.sync.dma_start(out=mem_planes[t][:], in_=mem_rows[:, t, :])
+        for q in range(4):
+            nc.sync.dma_start(
+                out=scale_table[32 * q : 32 * q + 4, :].bitcast(I32),
+                in_=x_scales[0, 4 * q : 4 * q + 4, :].bitcast(I32),
+            )
         nc.sync.dma_start(offs_t[:], offs)
-        mem_planes.append(load_plane(2))
-        r1_raw = [load_half(r1, "r1", 0)]
-        mem_planes.append(load_plane(3))
-        r1_raw.append(load_half(r1, "r1", 1))
-        load_words(0)
-        load_words(1)
-        w1_raw = [load_half(w1, "w1", a) for a in range(2)]
+        r1_raw = load_weight(r1, "r1")
+        word_table = keep.tile([P, T], I32, name="word_table")
+        nc.sync.dma_start(out=word_table[:], in_=x_words[0].rearrange("p n t -> p (n t)").bitcast(I32))
+        w1_raw = load_weight(w1, "w1")
         unit_t = keep.tile([P, PACK], F32, name="unit_t")
         nc.sync.dma_start(out=unit_t[:], in_=unit.rearrange("(p t) o -> p (t o)", t=PACK))
-        r2_raw = [load_half(r2, "r2", a) for a in range(2)]
-        w2_raw = [load_half(w2, "w2", a) for a in range(2)]
+        r2_raw = load_weight(r2, "r2")
+        w2_raw = load_weight(w2, "w2")
 
         gate_bank = [psum.tile([P, S], F32, name="gate_bank%d" % t) for t in range(PACK)]
         cand_bank = [psum.tile([P, S], F32, name="cand_bank%d" % t) for t in range(PACK)]
 
         old = keep.tile([P, PACK, S], F32, name="old")
-
-        def look_up(t):
+        for t in range(PACK):
             nc.vector.tensor_copy(old[:, t, :], mem_planes[t][:].indirect(slot_t[:]))
 
-        for t in range(3):
-            look_up(t)
+        half = S // 2
+        woven = []
+        for u, copy in enumerate((nc.vector.tensor_copy, nc.scalar.copy)):
+            tile = keep.tile([P, half, PACK], BF16, name="woven%d" % u, align_bytes=64)
+            copy(
+                out=tile[:].rearrange("p (c i) t -> p c t i", i=LINE),
+                in_=old[:, :, u * half : (u + 1) * half].rearrange("p t (c i) -> p c t i", i=LINE),
+            )
+            woven.append(tile[:].rearrange("p s t -> p (s t)"))
         x_scale = keep.tile([P, S], U8, name="x_scale", align_bytes=64)
         nc.vector.tensor_copy(x_scale[:], scale_table[:].indirect(offs_t[:]))
-        r1_dealt = dealt_tiles("r1")
-        deal(r1_dealt, r1_raw, 0, (1, 1))
-        look_up(3)
-        deal(r1_dealt, r1_raw, 1, (1, 1))
-
         old_mx = mx_tiles("old")
-        woven = []
         for u in range(2):
-            half = keep.tile([P, S // 2, PACK], BF16, name="woven%d" % u, tag=("woven0", "r1_raw1")[u], align_bytes=64)
-            copies[u](
-                out=half[:],
-                in_=old[:, :, u * 256 : (u + 1) * 256].rearrange("p t s -> p s t"),
-            )
-            woven.append(half)
-        r1_mx = quantize_weight("r1", r1_dealt)
-        for u in range(2):
-            quantize(old_mx, u * 256, (u + 1) * 256, woven[u][:].rearrange("p s t -> p (s t)"))
-        x_code = keep.tile([P, S], U32, name="x_code", tag="r1_raw1", align_bytes=64)
-        x_mx = (x_code, x_scale)
+            quantize(old_mx, u * half, woven[u])
+
+        r1_dealt = [deal(nc.scalar.copy, r1_raw, 0, "r1_low"), deal(nc.scalar.copy, r1_raw, 1, "r1_high")]
+        r1_mx = mx_tiles("r1")
+        quantize(r1_mx, 0, r1_dealt[0])
+        x_code = keep.tile([P, S], U32, name="x_code", align_bytes=64)
         nc.vector.tensor_copy(x_code[:], word_table[:].bitcast(U32).indirect(offs_t[:]))
+        x_mx = (x_code, x_scale)
+        quantize(r1_mx, 2 * P, r1_dealt[1])
         for t in range(PACK):
             product(gate_bank[t], t, r1_mx, old_mx, True)
 
-        w1_dealt = dealt_tiles("w1")
-        for a in range(2):
-            deal(w1_dealt, w1_raw, a)
-        w1_mx = quantize_weight("w1", w1_dealt)
+        w1_dealt = [deal(nc.vector.tensor_copy, w1_raw, 0, "w1_low"), deal(nc.scalar.copy, w1_raw, 1, "w1_high")]
+        w1_mx = mx_tiles("w1")
+        for u in range(PAIRS):
+            quantize(w1_mx, 2 * P * u, w1_dealt[u])
 
         gate, kept = {}, {}
-        gate_tag = ["gate0", "gate1", "w2_raw0", "w2_raw1"]
-        kept_tag = ["kept0", "kept1", "w2_dealt0", "w2_dealt1"]
 
-        def open_gate(t):
+        def open_gate(t, tag):
             product(gate_bank[t], t, w1_mx, x_mx, False)
-            gate[t] = keep.tile([P, S], F32, name="gate%d" % t, tag=gate_tag[t], align_bytes=64)
+            gate[t] = keep.tile([P, S], F32, name="gate", tag=tag, align_bytes=64)
             nc.scalar.activation(out=gate[t][:], in_=gate_bank[t][:], func=ACT.Sigmoid)
 
-        def forget(t):
-            kept[t] = keep.tile([P, S], F32, name="kept%d" % t, tag=kept_tag[t], align_bytes=64)
+        def forget(t, tag):
+            kept[t] = keep.tile([P, S], F32, name="kept", tag=tag, align_bytes=64)
             nc.vector.scalar_tensor_tensor(
                 out=kept[t][:], in0=old[:, t, :], scalar=unit_t[:, t : t + 1], in1=gate[t][:], op0=ALU.mult, op1=ALU.mult
             )
 
-        r2_dealt = dealt_tiles("r2")
-        deal(r2_dealt, r2_raw, 0, (0, 0))
-        open_gate(0)
-        deal(r2_dealt, r2_raw, 1)
-        forget(0)
-        r2_mx = quantize_weight("r2", r2_dealt)
-        open_gate(1)
-        for t in range(PACK):
+        open_gate(0, "gate0")
+        open_gate(1, "gate1")
+        open_gate(2, "gate2")
+        r2_low = deal(nc.vector.tensor_copy, r2_raw, 0, "w1_high")
+        forget(0, "kept0")
+        r2_high = deal(nc.scalar.copy, r2_raw, 1, "gate0")
+        r2_mx = mx_tiles("r2")
+        quantize(r2_mx, 0, r2_low)
+        for t in range(2):
             product(cand_bank[t], t, r2_mx, old_mx, True)
-        forget(1)
-        w2_dealt = dealt_tiles("w2")
-        deal(w2_dealt, w2_raw, 0, (1, 1))
-        open_gate(2)
-        deal(w2_dealt, w2_raw, 1)
-        w2_mx = quantize_weight("w2", w2_dealt, True)
-        open_gate(3)
-        forget(2)
-        forget(3)
+        forget(1, "kept1")
+        w2_dealt = [deal(nc.vector.tensor_copy, w2_raw, 0, "w1_high"), deal(nc.scalar.copy, w2_raw, 1, "gate1")]
+        quantize(r2_mx, 2 * P, r2_high)
+        for t in range(2, PACK):
+            product(cand_bank[t], t, r2_mx, old_mx, True)
+        w2_mx = mx_tiles("w2")
+        for t in range(PACK):
+            quantize(w2_mx, P * t, w2_dealt[t // 2][:, (t % 2) * PACK * P : (t % 2 + 1) * PACK * P])
+        open_gate(3, "w2_raw")
+        forget(2, "w1_high")
+        forget(3, "gate1")
 
         out_rows = out.rearrange("(p t) s -> p t s", t=PACK)
         for t in range(PACK):

@@ -12,39 +12,44 @@ U32 = mybir.dt.uint32
 U16 = mybir.dt.uint16
 U8 = mybir.dt.uint8
 FP8X4 = mybir.dt.float8_e4m3fn_x4
-ACT = mybir.ActivationFunctionType
+TANH = mybir.ActivationFunctionType.Tanh
 ALU = mybir.AluOpType
 
 P = 128
 PACK = 4
-PAIRS = 2
-LINE = 4
+PAIR = 2
+QUADRANT = 32
+GROUP = 16
+RUN = 4
+ALIGN = 64
+LOW, HIGH = 0, 1
 
 
 def tile_picked_ytgn_fg_p_kernel(
     tc, x_words, x_scales, mem, w1, w2, r1, r2, unit, offs, slot, out
 ):
     nc = tc.nc
+    on_vector, on_scalar = nc.vector.tensor_copy, nc.scalar.copy
     with ExitStack() as ctx:
         keep = ctx.enter_context(tc.tile_pool(name="keep", bufs=1))
         psum = ctx.enter_context(tc.psum_pool(name="psum", bufs=1))
 
         def load_weight(w, name):
-            raw = keep.tile([P, PACK, H], F32, name=name + "_raw", tag=name + "_raw", align_bytes=64)
+            raw = keep.tile([P, PACK, H], F32, name=name, tag=name, align_bytes=ALIGN)
             nc.sync.dma_start(out=raw[:], in_=w.rearrange("(p j) c -> p j c", j=PACK))
             return raw
 
-        def deal(copy, raw, u, tag):
-            dealt = keep.tile([P, 2, P, PACK], BF16, name="dealt", tag=tag, align_bytes=64)
+        def deal(copy, raw, pair, buffer):
+            dealt = keep.tile([P, PAIR, P, PACK], BF16, name="dealt", tag=buffer, align_bytes=ALIGN)
             copy(
                 out=dealt[:].rearrange("p v m j -> p m j v"),
-                in_=raw[:].rearrange("p j (m t) -> p m j t", t=PACK)[:, :, :, 2 * u : 2 * u + 2],
+                in_=raw[:].rearrange("p j (m t) -> p m j t", t=PACK)[:, :, :, PAIR * pair : PAIR * (pair + 1)],
             )
             return dealt[:].rearrange("p v m j -> p (v m j)")
 
         def mx_tiles(name):
-            codes = keep.tile([P, S], U32, name=name + "_codes", align_bytes=64)
-            scales = keep.tile([P, S], U8, name=name + "_scales", align_bytes=64)
+            codes = keep.tile([P, S], U32, name=name + "_codes", align_bytes=ALIGN)
+            scales = keep.tile([P, S], U8, name=name + "_scales", align_bytes=ALIGN)
             return codes, scales
 
         def quantize(mx, first, values):
@@ -63,34 +68,31 @@ def tile_picked_ytgn_fg_p_kernel(
                 stop=not start,
             )
 
-        offs_t = keep.tile([P, S // 16], U16, name="offs_t")
-        slot_t = keep.tile([P, S // 16], U16, name="slot_t")
+        unit_t = keep.tile([P, PACK], F32, name="unit_t")
+        nc.gpsimd.dma_start(out=unit_t[:], in_=unit.rearrange("(p t) o -> p (t o)", t=PACK))
+        half_unit = keep.tile([P, PACK], F32, name="half_unit")
+        nc.gpsimd.tensor_scalar_mul(half_unit[:], unit_t[:], 0.5)
+
+        offs_t = keep.tile([P, S // GROUP], U16, name="offs_t")
+        slot_t = keep.tile([P, S // GROUP], U16, name="slot_t")
         scale_table = keep.tile([P, T], U8, name="scale_table")
         nc.vector.memset(scale_table[:].bitcast(I32), 0)
-        warm = keep.tile([P, 8], F32, name="warm")
-        nc.vector.memset(warm[:], 0.0)
-        warm_out = keep.tile([P, 8], F32, name="warm_out")
-        nc.scalar.activation(out=warm_out[:], in_=warm[:], func=ACT.Sigmoid)
 
         mem_rows = mem.rearrange("(p t) u -> p t u", t=PACK)
         mem_planes = [keep.tile([P, U], F32, name="mem_plane%d" % t) for t in range(PACK)]
         nc.sync.dma_start(slot_t[:], slot)
         for t in range(PACK):
             nc.sync.dma_start(out=mem_planes[t][:], in_=mem_rows[:, t, :])
-        for q in range(4):
-            nc.sync.dma_start(
-                out=scale_table[32 * q : 32 * q + 4, :].bitcast(I32),
-                in_=x_scales[0, 4 * q : 4 * q + 4, :].bitcast(I32),
-            )
+        scale_rows = x_scales[0].bitcast(I32).rearrange("(q r) c -> r q c", r=PACK)
+        for r in range(PACK):
+            nc.sync.dma_start(out=scale_table[r:P:QUADRANT, :].bitcast(I32), in_=scale_rows[r])
         nc.sync.dma_start(offs_t[:], offs)
-        r1_raw = load_weight(r1, "r1")
+        r1_raw = load_weight(r1, "r1_raw")
         word_table = keep.tile([P, T], I32, name="word_table")
         nc.sync.dma_start(out=word_table[:], in_=x_words[0].rearrange("p n t -> p (n t)").bitcast(I32))
-        w1_raw = load_weight(w1, "w1")
-        unit_t = keep.tile([P, PACK], F32, name="unit_t")
-        nc.sync.dma_start(out=unit_t[:], in_=unit.rearrange("(p t) o -> p (t o)", t=PACK))
-        r2_raw = load_weight(r2, "r2")
-        w2_raw = load_weight(w2, "w2")
+        w1_raw = load_weight(w1, "w1_raw")
+        r2_raw = load_weight(r2, "r2_raw")
+        w2_raw = load_weight(w2, "w2_raw")
 
         gate_bank = [psum.tile([P, S], F32, name="gate_bank%d" % t) for t in range(PACK)]
         cand_bank = [psum.tile([P, S], F32, name="cand_bank%d" % t) for t in range(PACK)]
@@ -101,77 +103,88 @@ def tile_picked_ytgn_fg_p_kernel(
 
         half = S // 2
         woven = []
-        for u, copy in enumerate((nc.vector.tensor_copy, nc.scalar.copy)):
-            tile = keep.tile([P, half, PACK], BF16, name="woven%d" % u, align_bytes=64)
+        for u, copy in enumerate((on_vector, on_scalar)):
+            columns = keep.tile([P, half, PACK], BF16, name="woven%d" % u, align_bytes=ALIGN)
             copy(
-                out=tile[:].rearrange("p (c i) t -> p c t i", i=LINE),
-                in_=old[:, :, u * half : (u + 1) * half].rearrange("p t (c i) -> p c t i", i=LINE),
+                out=columns[:].rearrange("p (c i) t -> p c t i", i=RUN),
+                in_=old[:, :, u * half : (u + 1) * half].rearrange("p t (c i) -> p c t i", i=RUN),
             )
-            woven.append(tile[:].rearrange("p s t -> p (s t)"))
-        x_scale = keep.tile([P, S], U8, name="x_scale", align_bytes=64)
+            woven.append(columns[:].rearrange("p s t -> p (s t)"))
+        x_scale = keep.tile([P, S], U8, name="x_scale", align_bytes=ALIGN)
         nc.vector.tensor_copy(x_scale[:], scale_table[:].indirect(offs_t[:]))
         old_mx = mx_tiles("old")
-        for u in range(2):
+        for u in range(len(woven)):
             quantize(old_mx, u * half, woven[u])
 
-        r1_dealt = [deal(nc.scalar.copy, r1_raw, 0, "r1_low"), deal(nc.scalar.copy, r1_raw, 1, "r1_high")]
+        r1_low = deal(on_scalar, r1_raw, LOW, "r1_low")
+        r1_high = deal(on_scalar, r1_raw, HIGH, "r1_high")
         r1_mx = mx_tiles("r1")
-        quantize(r1_mx, 0, r1_dealt[0])
-        x_code = keep.tile([P, S], U32, name="x_code", align_bytes=64)
+        quantize(r1_mx, 0, r1_low)
+        x_code = keep.tile([P, S], U32, name="x_code", align_bytes=ALIGN)
         nc.vector.tensor_copy(x_code[:], word_table[:].bitcast(U32).indirect(offs_t[:]))
         x_mx = (x_code, x_scale)
-        quantize(r1_mx, 2 * P, r1_dealt[1])
+        quantize(r1_mx, PAIR * P, r1_high)
         for t in range(PACK):
             product(gate_bank[t], t, r1_mx, old_mx, True)
 
-        w1_dealt = [deal(nc.vector.tensor_copy, w1_raw, 0, "w1_low"), deal(nc.scalar.copy, w1_raw, 1, "w1_high")]
+        w1_low = deal(on_vector, w1_raw, LOW, "stage_a")
+        w1_high = deal(on_scalar, w1_raw, HIGH, "stage_b")
         w1_mx = mx_tiles("w1")
-        for u in range(PAIRS):
-            quantize(w1_mx, 2 * P * u, w1_dealt[u])
+        quantize(w1_mx, 0, w1_low)
+        quantize(w1_mx, PAIR * P, w1_high)
 
         gate, kept = {}, {}
 
-        def open_gate(t, tag):
+        def close_gate(t, buffer):
             product(gate_bank[t], t, w1_mx, x_mx, False)
-            gate[t] = keep.tile([P, S], F32, name="gate", tag=tag, align_bytes=64)
-            nc.scalar.activation(out=gate[t][:], in_=gate_bank[t][:], func=ACT.Sigmoid)
+            gate[t] = keep.tile([P, S], F32, name="gate", tag=buffer, align_bytes=ALIGN)
+            nc.scalar.activation(out=gate[t][:], in_=gate_bank[t][:], func=TANH, scale=0.5)
 
-        def forget(t, tag):
-            kept[t] = keep.tile([P, S], F32, name="kept", tag=tag, align_bytes=64)
+        def forget(t, buffer):
+            kept[t] = keep.tile([P, S], F32, name="kept", tag=buffer, align_bytes=ALIGN)
             nc.vector.scalar_tensor_tensor(
-                out=kept[t][:], in0=old[:, t, :], scalar=unit_t[:, t : t + 1], in1=gate[t][:], op0=ALU.mult, op1=ALU.mult
+                out=kept[t][:], in0=gate[t][:], scalar=1.0, in1=old[:, t, :], op0=ALU.add, op1=ALU.mult
             )
 
-        open_gate(0, "gate0")
-        open_gate(1, "gate1")
-        open_gate(2, "gate2")
-        r2_low = deal(nc.vector.tensor_copy, r2_raw, 0, "w1_high")
-        forget(0, "kept0")
-        r2_high = deal(nc.scalar.copy, r2_raw, 1, "gate0")
+        close_gate(0, "stage_c")
+        r2_low = deal(on_vector, r2_raw, LOW, "stage_b")
+        r2_high = deal(on_scalar, r2_raw, HIGH, "stage_a")
         r2_mx = mx_tiles("r2")
         quantize(r2_mx, 0, r2_low)
-        for t in range(2):
+        quantize(r2_mx, PAIR * P, r2_high)
+        for t in range(PACK):
             product(cand_bank[t], t, r2_mx, old_mx, True)
+        forget(0, "kept0")
+        close_gate(1, "gate1")
+        w2_low = deal(on_vector, w2_raw, LOW, "stage_b")
+        w2_high = deal(on_scalar, w2_raw, HIGH, "stage_c")
         forget(1, "kept1")
-        w2_dealt = [deal(nc.vector.tensor_copy, w2_raw, 0, "w1_high"), deal(nc.scalar.copy, w2_raw, 1, "gate1")]
-        quantize(r2_mx, 2 * P, r2_high)
-        for t in range(2, PACK):
-            product(cand_bank[t], t, r2_mx, old_mx, True)
+        close_gate(2, "gate2")
+
         w2_mx = mx_tiles("w2")
         for t in range(PACK):
-            quantize(w2_mx, P * t, w2_dealt[t // 2][:, (t % 2) * PACK * P : (t % 2 + 1) * PACK * P])
-        open_gate(3, "w2_raw")
-        forget(2, "w1_high")
-        forget(3, "gate1")
+            first = (t % PAIR) * P * PACK
+            quantize(w2_mx, t * P, (w2_low, w2_high)[t // PAIR][:, first : first + P * PACK])
+            product(cand_bank[t], t, w2_mx, x_mx, False)
+        close_gate(3, "w2_raw")
+        forget(2, "stage_b")
+        forget(3, "stage_c")
 
         out_rows = out.rearrange("(p t) s -> p t s", t=PACK)
         for t in range(PACK):
-            product(cand_bank[t], t, w2_mx, x_mx, False)
             cand = keep.tile([P, S], F32, name="cand%d" % t)
-            nc.scalar.activation(out=cand[:], in_=cand_bank[t][:], func=ACT.Tanh)
+            nc.scalar.activation(out=cand[:], in_=cand_bank[t][:], func=TANH)
             pieces = 2 if t == PACK - 1 else 1
+            width = S // pieces
             for a in range(pieces):
-                cols = slice(a * S // pieces, (a + 1) * S // pieces)
-                res = keep.tile([P, S // pieces], F32, name="res%d_%d" % (t, a))
-                nc.vector.tensor_tensor(out=res[:], in0=kept[t][:, cols], in1=cand[:, cols], op=ALU.add)
+                cols = slice(a * width, (a + 1) * width)
+                res = keep.tile([P, width], F32, name="res%d_%d" % (t, a))
+                nc.vector.scalar_tensor_tensor(
+                    out=res[:],
+                    in0=kept[t][:, cols],
+                    scalar=half_unit[:, t : t + 1],
+                    in1=cand[:, cols],
+                    op0=ALU.mult,
+                    op1=ALU.add,
+                )
                 nc.sync.dma_start(out=out_rows[:, t, cols], in_=res[:])

from contextlib import ExitStack

import concourse.mybir as mybir

K, T, S, H, U = 512, 2048, 512, 512, 1024
FLOPS = 4 * 2 * K * H * S

F32 = mybir.dt.float32
BF16 = mybir.dt.bfloat16
I32 = mybir.dt.int32
U32 = mybir.dt.uint32
U16 = mybir.dt.uint16
U8 = mybir.dt.uint8
FP8X4 = mybir.dt.float8_e4m3fn_x4
TANH = mybir.ActivationFunctionType.Tanh
ALU = mybir.AluOpType

P = 128
PACK = 4
PAIR = 2
QUADRANT = 32
GROUP = 16
RUN = 4
ALIGN = 64
LOW, HIGH = 0, 1


def tile_picked_ytgn_fg_p_kernel(
    tc, x_words, x_scales, mem, w1, w2, r1, r2, unit, offs, slot, out
):
    nc = tc.nc
    on_vector, on_scalar = nc.vector.tensor_copy, nc.scalar.copy
    with ExitStack() as ctx:
        keep = ctx.enter_context(tc.tile_pool(name="keep", bufs=1))
        psum = ctx.enter_context(tc.psum_pool(name="psum", bufs=1))

        def load_weight(w, name):
            raw = keep.tile([P, PACK, H], F32, name=name, tag=name, align_bytes=ALIGN)
            nc.sync.dma_start(out=raw[:], in_=w.rearrange("(p j) c -> p j c", j=PACK))
            return raw

        def deal(copy, raw, pair, buffer):
            dealt = keep.tile([P, PAIR, P, PACK], BF16, name="dealt", tag=buffer, align_bytes=ALIGN)
            copy(
                out=dealt[:].rearrange("p v m j -> p m j v"),
                in_=raw[:].rearrange("p j (m t) -> p m j t", t=PACK)[:, :, :, PAIR * pair : PAIR * (pair + 1)],
            )
            return dealt[:].rearrange("p v m j -> p (v m j)")

        def mx_tiles(name):
            codes = keep.tile([P, S], U32, name=name + "_codes", align_bytes=ALIGN)
            scales = keep.tile([P, S], U8, name=name + "_scales", align_bytes=ALIGN)
            return codes, scales

        def quantize(mx, first, values):
            cols = slice(first, first + values.shape[1] // PACK)
            nc.vector.quantize_mx(out=mx[0][:, cols].bitcast(FP8X4), scales=mx[1][:, cols], in_=values)

        def product(bank, t, weight, moving, start):
            cols = slice(t * P, (t + 1) * P)
            nc.tensor.matmul_mx(
                out=bank[:],
                lhsT=weight[0][:, cols].bitcast(FP8X4),
                lhsT_scale=weight[1][:, cols],
                rhs=moving[0][:].bitcast(FP8X4),
                rhs_scale=moving[1][:],
                start=start,
                stop=not start,
            )

        unit_t = keep.tile([P, PACK], F32, name="unit_t")
        nc.gpsimd.dma_start(out=unit_t[:], in_=unit.rearrange("(p t) o -> p (t o)", t=PACK))
        half_unit = keep.tile([P, PACK], F32, name="half_unit")
        nc.gpsimd.tensor_scalar_mul(half_unit[:], unit_t[:], 0.5)

        offs_t = keep.tile([P, S // GROUP], U16, name="offs_t")
        slot_t = keep.tile([P, S // GROUP], U16, name="slot_t")
        scale_table = keep.tile([P, T], U8, name="scale_table")
        nc.vector.memset(scale_table[:].bitcast(I32), 0)

        mem_rows = mem.rearrange("(p t) u -> p t u", t=PACK)
        mem_planes = [keep.tile([P, U], F32, name="mem_plane%d" % t) for t in range(PACK)]
        nc.sync.dma_start(slot_t[:], slot)
        for t in range(PACK):
            nc.sync.dma_start(out=mem_planes[t][:], in_=mem_rows[:, t, :])
        scale_rows = x_scales[0].bitcast(I32).rearrange("(q r) c -> r q c", r=PACK)
        for r in range(PACK):
            nc.sync.dma_start(out=scale_table[r:P:QUADRANT, :].bitcast(I32), in_=scale_rows[r])
        nc.sync.dma_start(offs_t[:], offs)
        r1_raw = load_weight(r1, "r1_raw")
        word_table = keep.tile([P, T], I32, name="word_table")
        nc.sync.dma_start(out=word_table[:], in_=x_words[0].rearrange("p n t -> p (n t)").bitcast(I32))
        w1_raw = load_weight(w1, "w1_raw")
        r2_raw = load_weight(r2, "r2_raw")
        w2_raw = load_weight(w2, "w2_raw")

        gate_bank = [psum.tile([P, S], F32, name="gate_bank%d" % t) for t in range(PACK)]
        cand_bank = [psum.tile([P, S], F32, name="cand_bank%d" % t) for t in range(PACK)]

        old = keep.tile([P, PACK, S], F32, name="old")
        for t in range(PACK):
            nc.vector.tensor_copy(old[:, t, :], mem_planes[t][:].indirect(slot_t[:]))

        half = S // 2
        woven = []
        for u, copy in enumerate((on_vector, on_scalar)):
            columns = keep.tile([P, half, PACK], BF16, name="woven%d" % u, align_bytes=ALIGN)
            copy(
                out=columns[:].rearrange("p (c i) t -> p c t i", i=RUN),
                in_=old[:, :, u * half : (u + 1) * half].rearrange("p t (c i) -> p c t i", i=RUN),
            )
            woven.append(columns[:].rearrange("p s t -> p (s t)"))
        x_scale = keep.tile([P, S], U8, name="x_scale", align_bytes=ALIGN)
        nc.vector.tensor_copy(x_scale[:], scale_table[:].indirect(offs_t[:]))
        old_mx = mx_tiles("old")
        for u in range(len(woven)):
            quantize(old_mx, u * half, woven[u])

        r1_low = deal(on_scalar, r1_raw, LOW, "r1_low")
        r1_high = deal(on_scalar, r1_raw, HIGH, "r1_high")
        r1_mx = mx_tiles("r1")
        quantize(r1_mx, 0, r1_low)
        x_code = keep.tile([P, S], U32, name="x_code", align_bytes=ALIGN)
        nc.vector.tensor_copy(x_code[:], word_table[:].bitcast(U32).indirect(offs_t[:]))
        x_mx = (x_code, x_scale)
        quantize(r1_mx, PAIR * P, r1_high)
        for t in range(PACK):
            product(gate_bank[t], t, r1_mx, old_mx, True)

        w1_low = deal(on_vector, w1_raw, LOW, "stage_a")
        w1_high = deal(on_scalar, w1_raw, HIGH, "stage_b")
        w1_mx = mx_tiles("w1")
        quantize(w1_mx, 0, w1_low)
        quantize(w1_mx, PAIR * P, w1_high)

        gate, kept = {}, {}

        def close_gate(t, buffer):
            product(gate_bank[t], t, w1_mx, x_mx, False)
            gate[t] = keep.tile([P, S], F32, name="gate", tag=buffer, align_bytes=ALIGN)
            nc.scalar.activation(out=gate[t][:], in_=gate_bank[t][:], func=TANH, scale=0.5)

        def forget(t, buffer):
            kept[t] = keep.tile([P, S], F32, name="kept", tag=buffer, align_bytes=ALIGN)
            nc.vector.scalar_tensor_tensor(
                out=kept[t][:], in0=gate[t][:], scalar=1.0, in1=old[:, t, :], op0=ALU.add, op1=ALU.mult
            )

        close_gate(0, "stage_c")
        r2_low = deal(on_vector, r2_raw, LOW, "stage_b")
        r2_high = deal(on_scalar, r2_raw, HIGH, "stage_a")
        r2_mx = mx_tiles("r2")
        quantize(r2_mx, 0, r2_low)
        quantize(r2_mx, PAIR * P, r2_high)
        for t in range(PACK):
            product(cand_bank[t], t, r2_mx, old_mx, True)
        forget(0, "kept0")
        close_gate(1, "gate1")
        w2_low = deal(on_vector, w2_raw, LOW, "stage_b")
        w2_high = deal(on_scalar, w2_raw, HIGH, "stage_c")
        forget(1, "kept1")
        close_gate(2, "gate2")

        w2_mx = mx_tiles("w2")
        for t in range(PACK):
            first = (t % PAIR) * P * PACK
            quantize(w2_mx, t * P, (w2_low, w2_high)[t // PAIR][:, first : first + P * PACK])
            product(cand_bank[t], t, w2_mx, x_mx, False)
        close_gate(3, "w2_raw")
        forget(2, "stage_b")
        forget(3, "stage_c")

        out_rows = out.rearrange("(p t) s -> p t s", t=PACK)
        for t in range(PACK):
            cand = keep.tile([P, S], F32, name="cand%d" % t)
            nc.scalar.activation(out=cand[:], in_=cand_bank[t][:], func=TANH)
            pieces = 2 if t == PACK - 1 else 1
            width = S // pieces
            for a in range(pieces):
                cols = slice(a * width, (a + 1) * width)
                res = keep.tile([P, width], F32, name="res%d_%d" % (t, a))
                nc.vector.scalar_tensor_tensor(
                    out=res[:],
                    in0=kept[t][:, cols],
                    scalar=half_unit[:, t : t + 1],
                    in1=cand[:, cols],
                    op0=ALU.mult,
                    op1=ALU.add,
                )
                nc.sync.dma_start(out=out_rows[:, t, cols], in_=res[:])
